import numpy as np
import ml_dtypes


def mxq(x, axis, fmt="e4m3"):
    dtype, down = {"e4m3": (ml_dtypes.float8_e4m3fn, 7), "e5m2": (ml_dtypes.float8_e5m2, 14)}[fmt]
    v = np.moveaxis(np.asarray(x, np.float32).astype(ml_dtypes.bfloat16).astype(np.float64), axis, -1)
    blocks = v.reshape(v.shape[:-1] + (-1, 32))
    amax = np.abs(blocks).max(-1, keepdims=True)
    byte = np.maximum(np.where(amax > 0, np.frexp(amax)[1] - 1 + 127, 0) - down, 1)
    scale = np.exp2(byte - 127.0)
    codes = (blocks / scale).astype(np.float32).astype(dtype).astype(np.float64)
    return np.moveaxis((codes * scale).reshape(v.shape), -1, axis)


WIDE = False


def mx_kscale(k):
    if not WIDE:
        return np.ones(k)
    levels = np.array([10, -10, 5, -5, 0])
    if k % 512:
        return np.exp2(np.random.permutation(np.resize(levels, k // 32))).repeat(32)
    a = np.empty((k // 512, 16))
    for p in range(k // 512):
        a[p, :8] = np.random.permutation(np.resize(levels, 8))
        for g in range(8):
            far = levels[np.abs(levels - a[p, g]) >= 10]
            a[p, g + 8] = far[np.random.randint(len(far))]
    return np.exp2(a.ravel()).repeat(32)


def f64(x):
    return np.asarray(x).astype(np.float64)


def striped(idx):
    return np.tile(idx.reshape(-1, 16).T, (8, 1)).astype(np.uint16)


def unstriped(offs):
    return offs[:16].T.reshape(-1).astype(np.int64)


E2M1 = np.array([0.0, 0.5, 1.0, 1.5, 2.0, 3.0, 4.0, 6.0, -0.0, -0.5, -1.0, -1.5, -2.0, -3.0, -4.0, -6.0])


def pack_weight(w, fmt):
    k, n = w.shape
    w = f64(np.asarray(w, np.float32).astype(ml_dtypes.bfloat16)).reshape(k // 32, 32, n)
    amax = np.abs(w).max(1)
    if fmt == "e4m3":
        byte = np.frexp(amax)[1] - 1 + 127 - 7
    else:
        mant, ex = np.frexp(amax / 6.0)
        byte = np.where(mant > 0.5, ex, ex - 1) + 127
    byte = np.clip(np.where(amax > 0, byte, 1), 1, 254)
    scaled = (w * np.exp2(127.0 - byte)[:, None, :]).reshape(k, n).astype(np.float32)
    by_word = np.ascontiguousarray(scaled.reshape(k // 512, 128, 4, n).transpose(0, 1, 3, 2))
    if fmt == "e4m3":
        words = by_word.astype(ml_dtypes.float8_e4m3fn).view(np.uint8)
    else:
        c = by_word.astype(ml_dtypes.float4_e2m1fn).view(np.uint8) & 0xF
        words = (c[..., 0::2] | (c[..., 1::2] << 4)).reshape(k // 512, 128, 2 * n)
    return np.ascontiguousarray(words), np.ascontiguousarray(byte.astype(np.uint8).reshape(k // 512, 16, n))


def unpack_weight(words, scales, fmt):
    g, _, n = scales.shape
    words = np.ascontiguousarray(words).reshape(g, 128, n, -1)
    if fmt == "e4m3":
        vals = words.view(ml_dtypes.float8_e4m3fn).astype(np.float64)
    else:
        nib = np.empty((g, 128, n, 4), np.uint8)
        nib[..., 0::2] = words & 0xF
        nib[..., 1::2] = words >> 4
        vals = E2M1[nib]
    vals = vals * np.repeat(np.exp2(scales.astype(np.float64) - 127.0), 8, axis=1)[..., None]
    return vals.transpose(0, 1, 3, 2).reshape(g * 512, n)


def gelu(v):
    return 0.5 * v * (1.0 + np.tanh(np.sqrt(2.0 / np.pi) * (v + 0.044715 * v**3)))


K, T, S, H, P, P2, N = 1024, 4096, 1024, 1024, 512, 256, 768

def setup_inputs():
    n = np.random.standard_normal
    s = mx_kscale(K)[:, None]
    u = mx_kscale(H)[:, None]
    tab_words, tab_scales = pack_weight(n((K, T)) * s, "e4m3")
    w2_words, w2_scales = pack_weight(n((K, H)) / np.sqrt(K) / s, "e2m1")
    return {
        "tab_words": tab_words, "tab_scales": tab_scales,
        "w1": (1.3 * n((K, H)) / np.sqrt(K) / s).astype(np.float32),
        "w2_words": w2_words, "w2_scales": w2_scales,
        "gain": (np.exp(0.3 * n(H)) * u[:, 0]).astype(np.float32),
        "wo": (n((H, N)) / np.sqrt(H) / u).astype(np.float32),
        "offs": striped(np.random.permutation(T)[:S]),
        "pos1": striped(np.random.permutation(S)[:P]),
        "pos2": striped(np.random.permutation(S)[:P]),
        "pos3": striped(np.random.permutation(P)[:P2]),
        "pos4": striped(np.random.permutation(P)[:P2]),
    }

def reference(tab_words, tab_scales, w1, w2_words, w2_scales, gain, wo, offs, pos1, pos2, pos3, pos4):
    v = unpack_weight(tab_words, tab_scales, "e4m3")[:, unstriped(offs)]
    w2 = unpack_weight(w2_words, w2_scales, "e2m1")
    a = mxq(f64(w1), 0, "e4m3").T @ v
    b = w2.T @ v
    h = (np.tanh(a) * b + np.abs(a)) * f64(gain)[:, None]
    z = np.minimum(h[:, unstriped(pos1)], h[:, unstriped(pos2)])
    y = mxq(f64(wo), 0, "e4m3").T @ mxq(z, 0, "e4m3")
    return np.maximum(y[:, unstriped(pos3)], y[:, unstriped(pos4)])

@@ -1,0 +1,262 @@
+from contextlib import ExitStack
+
+import concourse.mybir as mybir
+from concourse.masks import make_identity
+
+K, T, S, H, PAIRS, OUTS, N = 1024, 4096, 1024, 1024, 512, 256, 768
+FLOPS = 2 * (2 * K * H * S + H * N * PAIRS)
+
+F32 = mybir.dt.float32
+BF16 = mybir.dt.bfloat16
+I32 = mybir.dt.int32
+U32 = mybir.dt.uint32
+U16 = mybir.dt.uint16
+U8 = mybir.dt.uint8
+FP8X4 = mybir.dt.float8_e4m3fn_x4
+FP4X4 = mybir.dt.float4_e2m1fn_x4
+ALU = mybir.AluOpType
+ACT = mybir.ActivationFunctionType
+
+P = 128
+PACK = 4
+PASS = P * PACK
+BANK = 512
+WO_COLS = 256
+
+
+def tile_list_seedling_lifting_gauge_kernel(
+    tc, tab_words, tab_scales, w1, w2_words, w2_scales, gain, wo, offs, pos1, pos2, pos3, pos4, out
+):
+    nc = tc.nc
+    with ExitStack() as ctx:
+        lists = ctx.enter_context(tc.tile_pool(name="lists", bufs=1))
+        keep = ctx.enter_context(tc.tile_pool(name="keep", bufs=1))
+        ring = ctx.enter_context(tc.tile_pool(name="ring", bufs=2))
+        psum = ctx.enter_context(tc.psum_pool(name="psum", bufs=8))
+
+        def load_list(src, name):
+            tile = lists.tile(list(src.shape), U16, name=name)
+            nc.sync.dma_start(tile[:], src)
+            return tile
+
+        def load_table(a):
+            tile = keep.tile([P, T], U32, name=f"tab_w{a}", tag=f"tab_w{a}")
+            nc.sync.dma_start(tile[:].bitcast(I32), tab_words[a].rearrange("p t i -> p (t i)").bitcast(I32))
+            return tile
+
+        def load_w1(a, b):
+            tile = ring.tile([P, PACK, PASS], F32, name="w1_raw", tag="raw")
+            rows = w1[a * PASS : (a + 1) * PASS, b * PASS : (b + 1) * PASS]
+            nc.sync.dma_start(tile[:], rows.rearrange("(p j) c -> p j c", j=PACK))
+            return tile
+
+        def load_w2(b):
+            tile = keep.tile([P, 2, 2 * PASS], U8, name="w2_raw")
+            cols = w2_words[:, :, 2 * b * PASS : 2 * (b + 1) * PASS]
+            nc.sync.dma_start(tile[:].bitcast(I32), cols.rearrange("a p c -> p a c").bitcast(I32))
+            return tile
+
+        def load_wo(b):
+            tile = ring.tile([P, PACK, N], F32, name="wo_raw", tag="raw")
+            rows = wo[b * PASS : (b + 1) * PASS, :].rearrange("(g t i) n -> t g i n", t=PACK, i=8)
+            for t in range(PACK):
+                nc.sync.dma_start(tile[:, t, :], rows[t])
+            return tile
+
+        gain_rows = keep.tile([P, P], F32, name="gain_rows", tag="tab_w1")
+        nc.vector.memset(gain_rows[:], 0.0)
+        for b in range(2):
+            nc.gpsimd.dma_start(
+                gain_rows[PACK * b : PACK * (b + 1), :].rearrange("t (g i) -> t g i", i=8),
+                gain[b * PASS : (b + 1) * PASS].rearrange("(g t i) -> t g i", t=PACK, i=8),
+            )
+        ident = keep.tile([P, P], F32, name="ident")
+        make_identity(nc, ident[:])
+        tab_s = keep.tile([P, T], U8, name="tab_s")
+        nc.vector.memset(tab_s[:].bitcast(I32), 0)
+        for q in range(4):
+            nc.scalar.dma_start(tab_s[32 * q : 32 * q + 8, :].bitcast(I32), tab_scales[:, 4 * q : 4 * q + 4, :].bitcast(I32))
+        w2_s_raw = keep.tile([P, 2, H], U8, name="w2_s_raw")
+        nc.vector.memset(w2_s_raw[:].bitcast(I32), 0)
+        for q in range(4):
+            nc.gpsimd.dma_start(
+                w2_s_raw[32 * q : 32 * q + 4, :, :].bitcast(I32),
+                w2_scales[:, 4 * q : 4 * q + 4, :].rearrange("a r c -> r a c").bitcast(I32),
+            )
+        v_s1 = keep.tile([P, S], U8, name="v_s1", align_bytes=64)
+        nc.vector.memset(v_s1[:].bitcast(I32), 0)
+
+        offs_t = load_list(offs, "offs_t")
+        pos1_t = load_list(pos1, "pos1_t")
+        pos2_t = load_list(pos2, "pos2_t")
+        pos3_t = load_list(pos3, "pos3_t")
+        pos4_t = load_list(pos4, "pos4_t")
+        tab_w = [load_table(0)]
+        w1_raw = {(a, 0): load_w1(a, 0) for a in range(2)}
+        w2_raw = [load_w2(0)]
+        wo_raw = []
+
+        gain_ps = psum.tile([P, BANK], F32, name="bank")
+        nc.tensor.transpose(gain_ps[:, :P], gain_rows[:], ident[:])
+        gain_t = keep.tile([P, 8], F32, name="gain_t")
+        nc.scalar.copy(gain_t[:], gain_ps[:, :8])
+        tab_w.append(load_table(1))
+
+        v_w = [keep.tile([P, S], U32, name=f"v_w{a}", align_bytes=64) for a in range(2)]
+        nc.vector.tensor_copy(v_w[0][:], tab_w[0][:].indirect(offs_t[:]))
+        v_s0 = keep.tile([P, S], U8, name="v_s0", align_bytes=64)
+        nc.vector.tensor_copy(v_s0[:], tab_s[:].indirect(offs_t[:]))
+        for q in range(4):
+            nc.scalar.dma_start(v_s1[32 * q : 32 * q + 4, :].bitcast(I32), v_s0[32 * q + 4 : 32 * q + 8, :].bitcast(I32))
+        v_s = [v_s0, v_s1]
+
+        w1_c, w1_s, w2_c = {}, {}, {}
+
+        def prepare_w1(a, b):
+            grouped = ring.tile([P, PACK, PASS], BF16, name="w1_grouped", align_bytes=64)
+            src = w1_raw[a, b][:].rearrange("p j (g t u i) -> p t g u j i", t=PACK, u=2, i=4)
+            dst = grouped[:].rearrange("p t (g u i j) -> p t g u j i", u=2, i=4, j=PACK)
+            for t in range(PACK):
+                nc.scalar.copy(dst[:, t], src[:, t])
+            codes = keep.tile([P, PASS], U32, name=f"w1_c{a}{b}", align_bytes=64)
+            scales = keep.tile([P, PASS], U8, name=f"w1_s{a}{b}", align_bytes=64)
+            nc.vector.quantize_mx(codes[:].bitcast(FP8X4), scales[:], grouped[:].rearrange("p t c -> p (t c)"))
+            w1_c[a, b], w1_s[a, b] = codes, scales
+
+        def prepare_w2(b):
+            tile = keep.tile([P, 2, 2 * PASS], U8, name=f"w2_c{b}", align_bytes=64)
+            nc.vector.tensor_copy(
+                tile[:].bitcast(I32).rearrange("p a (t g w) -> p a t g w", t=PACK, w=4),
+                w2_raw[b][:].bitcast(I32).rearrange("p a (g t w) -> p a t g w", t=PACK, w=4),
+            )
+            w2_c[b] = tile
+
+        wo_c = [keep.tile([P, N], U32, name=f"wo_c{b}", align_bytes=64) for b in range(2)]
+        wo_s = [keep.tile([P, N], U8, name=f"wo_s{b}", align_bytes=64) for b in range(2)]
+
+        def prepare_wo(b, part):
+            cols = slice(part * WO_COLS, (part + 1) * WO_COLS)
+            grouped = ring.tile([P, WO_COLS, PACK], BF16, name="wo_grouped", align_bytes=64)
+            nc.scalar.copy(
+                grouped[:].rearrange("p (c i) t -> p c t i", i=4),
+                wo_raw[b][:, :, cols].rearrange("p t (c i) -> p c t i", i=4),
+            )
+            nc.vector.quantize_mx(
+                wo_c[b][:, cols].bitcast(FP8X4), wo_s[b][:, cols], grouped[:].rearrange("p c t -> p (c t)")
+            )
+
+        w2_s = keep.tile([P, 2, H], U8, name="w2_s", align_bytes=64)
+        nc.vector.tensor_copy(
+            w2_s[:].bitcast(I32).rearrange("p a (b t g w) -> p (a b) t g w", b=2, t=PACK, w=2),
+            w2_s_raw[:].bitcast(I32).rearrange("p a (b g t w) -> p (a b) t g w", b=2, t=PACK, w=2),
+        )
+        prepare_w1(0, 0)
+        prepare_w1(1, 0)
+        prepare_w2(0)
+        for a in range(2):
+            w1_raw[a, 1] = load_w1(a, 1)
+        w2_raw.append(load_w2(1))
+        for half in range(2):
+            nc.vector.tensor_copy(
+                v_w[1][:, half * BANK : (half + 1) * BANK], tab_w[1][:].indirect(offs_t[:, half * 32 : (half + 1) * 32])
+            )
+
+        def products(r):
+            b, t = divmod(r, PACK)
+            cols = slice(t * P, (t + 1) * P)
+            bent = ring.tile([P, S], F32, name="bent")
+            size = ring.tile([P, S], F32, name="size")
+            for half in range(2):
+                js = slice(half * BANK, (half + 1) * BANK)
+                a_ps = psum.tile([P, BANK], F32, name="bank")
+                for a in range(2):
+                    nc.tensor.matmul_mx(
+                        a_ps[:], lhsT=w1_c[a, b][:, cols].bitcast(FP8X4), lhsT_scale=w1_s[a, b][:, cols],
+                        rhs=v_w[a][:, js].bitcast(FP8X4), rhs_scale=v_s[a][:, js], start=a == 0, stop=a == 1,
+                    )
+                b_ps = psum.tile([P, BANK], F32, name="bank")
+                for a in range(2):
+                    nc.tensor.matmul_mx(
+                        b_ps[:], lhsT=w2_c[b][:, a, 2 * t * P : 2 * (t + 1) * P].bitcast(FP4X4),
+                        lhsT_scale=w2_s[:, a, r * P : (r + 1) * P],
+                        rhs=v_w[a][:, js].bitcast(FP8X4), rhs_scale=v_s[a][:, js], start=a == 0, stop=a == 1,
+                    )
+                nc.scalar.activation(bent[:, js], a_ps[:], ACT.Tanh)
+                nc.scalar.activation(size[:, js], a_ps[:], ACT.Abs)
+                nc.vector.scalar_tensor_tensor(bent[:, js], b_ps[:], gain_t[:, r : r + 1], bent[:, js], ALU.mult, ALU.mult)
+            return bent, size
+
+        def add_terms(r, bent, size):
+            h = ring.tile([P, S], F32, name="h")
+            nc.vector.scalar_tensor_tensor(h[:], size[:], gain_t[:, r : r + 1], bent[:], ALU.mult, ALU.add)
+            return h
+
+        z_c, z_s = {}, {}
+
+        def weaker(root, shoot):
+            z = ring.tile([P, PAIRS, PACK], BF16, name="z", align_bytes=64)
+            nc.vector.tensor_tensor(
+                z[:].rearrange("p (c i) t -> p c t i", i=4),
+                root[:].rearrange("p t (c i) -> p c t i", i=4),
+                shoot[:].rearrange("p t (c i) -> p c t i", i=4),
+                ALU.min,
+            )
+            return z
+
+        def quantise_z(b, z):
+            codes = keep.tile([P, PAIRS], U32, name=f"z_c{b}", align_bytes=64)
+            scales = keep.tile([P, PAIRS], U8, name=f"z_s{b}", align_bytes=64)
+            nc.vector.quantize_mx(codes[:].bitcast(FP8X4), scales[:], z[:].rearrange("p m t -> p (m t)"))
+            z_c[b], z_s[b] = codes, scales
+
+        views = {}
+        h_prev = None
+        z0 = None
+        for r in range(9):
+            if r < 8:
+                terms = products(r)
+            if r == 5:
+                z0 = weaker(*views[0])
+            if r > 0:
+                b, t = divmod(r - 1, PACK)
+                if t == 0:
+                    views[b] = (
+                        ring.tile([P, PACK, PAIRS], F32, name="root"),
+                        ring.tile([P, PACK, PAIRS], F32, name="shoot"),
+                    )
+                nc.vector.tensor_copy(views[b][0][:, t, :], h_prev[:].indirect(pos1_t[:]))
+            if r < 8:
+                h_next = add_terms(r, *terms)
+            if r > 0:
+                nc.vector.tensor_copy(views[b][1][:, t, :], h_prev[:].indirect(pos2_t[:]))
+            if r == 5:
+                quantise_z(0, z0)
+            h_prev = h_next
+            if r in (1, 2):
+                prepare_w1(r - 1, 1)
+                wo_raw.append(load_wo(r - 1))
+            if r == 2:
+                prepare_w2(1)
+            if 3 <= r < 6:
+                prepare_wo(0, r - 3)
+            if 5 <= r < 8:
+                prepare_wo(1, r - 5)
+        quantise_z(1, weaker(*views[1]))
+
+        for n in range(N // P):
+            cols = slice(n * P, (n + 1) * P)
+            y_ps = psum.tile([P, BANK], F32, name="bank")
+            for b in range(2):
+                nc.tensor.matmul_mx(
+                    y_ps[:], lhsT=wo_c[b][:, cols].bitcast(FP8X4), lhsT_scale=wo_s[b][:, cols],
+                    rhs=z_c[b][:].bitcast(FP8X4), rhs_scale=z_s[b][:], start=b == 0, stop=b == 1,
+                )
+            y = ring.tile([P, PAIRS], F32, name="y", bufs=3)
+            nc.scalar.copy(y[:], y_ps[:])
+            left = ring.tile([P, OUTS], F32, name="left")
+            right = ring.tile([P, OUTS], F32, name="right")
+            nc.vector.tensor_copy(left[:], y[:].indirect(pos3_t[:]))
+            nc.vector.tensor_copy(right[:], y[:].indirect(pos4_t[:]))
+            best = ring.tile([P, OUTS], F32, name="best", bufs=3)
+            nc.vector.tensor_tensor(best[:], left[:], right[:], ALU.max)
+            nc.sync.dma_start(out[cols, :], best[:])

@@ -24,6 +24,10 @@ BANK = 512
 WO_COLS = 256
 
 
+def turned(r, half):
+    return r > 0
+
+
 def tile_list_seedling_lifting_gauge_kernel(
     tc, tab_words, tab_scales, w1, w2_words, w2_scales, gain, wo, offs, pos1, pos2, pos3, pos4, out
 ):
@@ -44,8 +48,8 @@ def tile_list_seedling_lifting_gauge_kernel(
             nc.sync.dma_start(tile[:].bitcast(I32), tab_words[a].rearrange("p t i -> p (t i)").bitcast(I32))
             return tile
 
-        def load_w1(a, b):
-            tile = ring.tile([P, PACK, PASS], F32, name="w1_raw", tag="raw")
+        def load_w1(a, b, tag):
+            tile = keep.tile([P, PACK, PASS], F32, name="w1_raw", tag=tag)
             rows = w1[a * PASS : (a + 1) * PASS, b * PASS : (b + 1) * PASS]
             nc.sync.dma_start(tile[:], rows.rearrange("(p j) c -> p j c", j=PACK))
             return tile
@@ -57,7 +61,7 @@ def tile_list_seedling_lifting_gauge_kernel(
             return tile
 
         def load_wo(b):
-            tile = ring.tile([P, PACK, N], F32, name="wo_raw", tag="raw")
+            tile = keep.tile([P, PACK, N], F32, name="wo_raw", tag=f"stage{b}")
             rows = wo[b * PASS : (b + 1) * PASS, :].rearrange("(g t i) n -> t g i n", t=PACK, i=8)
             for t in range(PACK):
                 nc.sync.dma_start(tile[:, t, :], rows[t])
@@ -72,7 +76,7 @@ def tile_list_seedling_lifting_gauge_kernel(
             )
         ident = keep.tile([P, P], F32, name="ident")
         make_identity(nc, ident[:])
-        tab_s = keep.tile([P, T], U8, name="tab_s")
+        tab_s = keep.tile([P, T], U8, name="tab_s", tag="stage0")
         nc.vector.memset(tab_s[:].bitcast(I32), 0)
         for q in range(4):
             nc.scalar.dma_start(tab_s[32 * q : 32 * q + 8, :].bitcast(I32), tab_scales[:, 4 * q : 4 * q + 4, :].bitcast(I32))
@@ -92,7 +96,7 @@ def tile_list_seedling_lifting_gauge_kernel(
         pos3_t = load_list(pos3, "pos3_t")
         pos4_t = load_list(pos4, "pos4_t")
         tab_w = [load_table(0)]
-        w1_raw = {(a, 0): load_w1(a, 0) for a in range(2)}
+        w1_raw = {(0, 0): load_w1(0, 0, "first"), (1, 0): load_w1(1, 0, "stage1")}
         w2_raw = [load_w2(0)]
         wo_raw = []
 
@@ -107,7 +111,7 @@ def tile_list_seedling_lifting_gauge_kernel(
         v_s0 = keep.tile([P, S], U8, name="v_s0", align_bytes=64)
         nc.vector.tensor_copy(v_s0[:], tab_s[:].indirect(offs_t[:]))
         for q in range(4):
-            nc.scalar.dma_start(v_s1[32 * q : 32 * q + 4, :].bitcast(I32), v_s0[32 * q + 4 : 32 * q + 8, :].bitcast(I32))
+            nc.sync.dma_start(v_s1[32 * q : 32 * q + 4, :].bitcast(I32), v_s0[32 * q + 4 : 32 * q + 8, :].bitcast(I32))
         v_s = [v_s0, v_s1]
 
         w1_c, w1_s, w2_c = {}, {}, {}
@@ -154,42 +158,65 @@ def tile_list_seedling_lifting_gauge_kernel(
         prepare_w1(1, 0)
         prepare_w2(0)
         for a in range(2):
-            w1_raw[a, 1] = load_w1(a, 1)
+            w1_raw[a, 1] = load_w1(a, 1, f"stage{a}")
         w2_raw.append(load_w2(1))
         for half in range(2):
             nc.vector.tensor_copy(
                 v_w[1][:, half * BANK : (half + 1) * BANK], tab_w[1][:].indirect(offs_t[:, half * 32 : (half + 1) * 32])
             )
 
-        def products(r):
+        def operands(r, a):
             b, t = divmod(r, PACK)
             cols = slice(t * P, (t + 1) * P)
-            bent = ring.tile([P, S], F32, name="bent")
-            size = ring.tile([P, S], F32, name="size")
-            for half in range(2):
+            first = (w1_c[a, b][:, cols].bitcast(FP8X4), w1_s[a, b][:, cols])
+            second = (w2_c[b][:, a, 2 * t * P : 2 * (t + 1) * P].bitcast(FP4X4), w2_s[:, a, r * P : (r + 1) * P])
+            return first, second
+
+        def reading(r, half, which):
+            bank = psum.tile([P, BANK], F32, name="bank")
+            if turned(r, half):
+                for piece in range(BANK // P):
+                    js = slice(half * BANK + piece * P, half * BANK + (piece + 1) * P)
+                    for a in range(2):
+                        codes, scales = operands(r, a)[which]
+                        nc.tensor.matmul_mx(
+                            bank[:, piece * P : (piece + 1) * P], lhsT=v_w[a][:, js].bitcast(FP8X4), lhsT_scale=v_s[a][:, js],
+                            rhs=codes, rhs_scale=scales, start=a == 0, stop=a == 1,
+                        )
+            else:
                 js = slice(half * BANK, (half + 1) * BANK)
-                a_ps = psum.tile([P, BANK], F32, name="bank")
                 for a in range(2):
+                    codes, scales = operands(r, a)[which]
                     nc.tensor.matmul_mx(
-                        a_ps[:], lhsT=w1_c[a, b][:, cols].bitcast(FP8X4), lhsT_scale=w1_s[a, b][:, cols],
+                        bank[:], lhsT=codes, lhsT_scale=scales,
                         rhs=v_w[a][:, js].bitcast(FP8X4), rhs_scale=v_s[a][:, js], start=a == 0, stop=a == 1,
                     )
-                b_ps = psum.tile([P, BANK], F32, name="bank")
-                for a in range(2):
-                    nc.tensor.matmul_mx(
-                        b_ps[:], lhsT=w2_c[b][:, a, 2 * t * P : 2 * (t + 1) * P].bitcast(FP4X4),
-                        lhsT_scale=w2_s[:, a, r * P : (r + 1) * P],
-                        rhs=v_w[a][:, js].bitcast(FP8X4), rhs_scale=v_s[a][:, js], start=a == 0, stop=a == 1,
-                    )
-                nc.scalar.activation(bent[:, js], a_ps[:], ACT.Tanh)
-                nc.scalar.activation(size[:, js], a_ps[:], ACT.Abs)
-                nc.vector.scalar_tensor_tensor(bent[:, js], b_ps[:], gain_t[:, r : r + 1], bent[:, js], ALU.mult, ALU.mult)
+            return bank
+
+        def products(r, half):
+            bent = ring.tile([P, BANK], F32, name="bent", bufs=4)
+            size = ring.tile([P, BANK], F32, name="size", bufs=4)
+            a_ps = reading(r, half, 0)
+            b_ps = reading(r, half, 1)
+            nc.scalar.activation(bent[:], a_ps[:], ACT.Tanh)
+            nc.scalar.activation(size[:], a_ps[:], ACT.Abs)
+            if turned(r, half):
+                nc.vector.tensor_tensor(bent[:], b_ps[:], bent[:], ALU.mult)
+            else:
+                nc.vector.scalar_tensor_tensor(bent[:], b_ps[:], gain_t[:, r : r + 1], bent[:], ALU.mult, ALU.mult)
             return bent, size
 
-        def add_terms(r, bent, size):
-            h = ring.tile([P, S], F32, name="h")
-            nc.vector.scalar_tensor_tensor(h[:], size[:], gain_t[:, r : r + 1], bent[:], ALU.mult, ALU.add)
-            return h
+        def add_terms(r, half, h, bent, size):
+            js = slice(half * BANK, (half + 1) * BANK)
+            if turned(r, half):
+                bank = psum.tile([P, BANK], F32, name="bank")
+                for piece in range(BANK // P):
+                    cols = slice(piece * P, (piece + 1) * P)
+                    nc.tensor.matmul(bank[:, cols], lhsT=size[:, cols], rhs=ident[:], is_transpose=True, start=True, stop=False)
+                    nc.tensor.matmul(bank[:, cols], lhsT=bent[:, cols], rhs=ident[:], is_transpose=True, start=False, stop=True)
+                nc.scalar.activation(h[:, js], bank[:], ACT.Copy, scale=gain_t[:, r : r + 1])
+            else:
+                nc.vector.scalar_tensor_tensor(h[:, js], size[:], gain_t[:, r : r + 1], bent[:], ALU.mult, ALU.add)
 
         z_c, z_s = {}, {}
 
@@ -209,39 +236,37 @@ def tile_list_seedling_lifting_gauge_kernel(
             nc.vector.quantize_mx(codes[:].bitcast(FP8X4), scales[:], z[:].rearrange("p m t -> p (m t)"))
             z_c[b], z_s[b] = codes, scales
 
-        views = {}
-        h_prev = None
+        views, hs, terms = {}, {}, {}
+
+        def pick(r, side):
+            b, t = divmod(r, PACK)
+            if t == 0:
+                views[b, side] = ring.tile([P, PACK, PAIRS], F32, name=f"view{side}")
+            nc.vector.tensor_copy(views[b, side][:, t, :], hs[r][:].indirect((pos1_t, pos2_t)[side][:]))
+
         z0 = None
-        for r in range(9):
-            if r < 8:
-                terms = products(r)
-            if r == 5:
-                z0 = weaker(*views[0])
-            if r > 0:
-                b, t = divmod(r - 1, PACK)
-                if t == 0:
-                    views[b] = (
-                        ring.tile([P, PACK, PAIRS], F32, name="root"),
-                        ring.tile([P, PACK, PAIRS], F32, name="shoot"),
-                    )
-                nc.vector.tensor_copy(views[b][0][:, t, :], h_prev[:].indirect(pos1_t[:]))
-            if r < 8:
-                h_next = add_terms(r, *terms)
-            if r > 0:
-                nc.vector.tensor_copy(views[b][1][:, t, :], h_prev[:].indirect(pos2_t[:]))
-            if r == 5:
+        for step in range(10):
+            for half in range(2):
+                if step < 8:
+                    terms[step, half] = products(step, half)
+                if 1 <= step < 9:
+                    if half == 0:
+                        hs[step - 1] = ring.tile([P, S], F32, name="h", bufs=3)
+                    add_terms(step - 1, half, hs[step - 1], *terms[step - 1, half])
+                if 2 <= step:
+                    pick(step - 2, half)
+            if step == 6:
+                z0 = weaker(views[0, 0], views[0, 1])
+            if step == 7:
                 quantise_z(0, z0)
-            h_prev = h_next
-            if r in (1, 2):
-                prepare_w1(r - 1, 1)
-                wo_raw.append(load_wo(r - 1))
-            if r == 2:
+            if step in (1, 2):
+                prepare_w1(step - 1, 1)
+                wo_raw.append(load_wo(step - 1))
+            if step == 2:
                 prepare_w2(1)
-            if 3 <= r < 6:
-                prepare_wo(0, r - 3)
-            if 5 <= r < 8:
-                prepare_wo(1, r - 5)
-        quantise_z(1, weaker(*views[1]))
+            if 3 <= step < 9:
+                prepare_wo(*divmod(step - 3, 3))
+        quantise_z(1, weaker(views[1, 0], views[1, 1]))
 
         for n in range(N // P):
             cols = slice(n * P, (n + 1) * P)

@@ -20,12 +20,15 @@ ACT = mybir.ActivationFunctionType
 P = 128
 PACK = 4
 PASS = P * PACK
+RUN = 8
+QUADS = 4
 BANK = 512
+LINE = 4
+ROW_TILES = H // P
+OUT_TILES = N // P
 WO_COLS = 256
-
-
-def turned(r, half):
-    return r > 0
+PLAIN_TILES = 2
+W1_AHEAD = 2
 
 
 def tile_list_seedling_lifting_gauge_kernel(
@@ -38,250 +41,259 @@ def tile_list_seedling_lifting_gauge_kernel(
         ring = ctx.enter_context(tc.tile_pool(name="ring", bufs=2))
         psum = ctx.enter_context(tc.psum_pool(name="psum", bufs=8))
 
+
+        def paced(shape, dtype):
+            return ring.tile(shape, dtype, name="paced", bufs=5, align_bytes=64)
+
         def load_list(src, name):
             tile = lists.tile(list(src.shape), U16, name=name)
             nc.sync.dma_start(tile[:], src)
             return tile
 
-        def load_table(a):
-            tile = keep.tile([P, T], U32, name=f"tab_w{a}", tag=f"tab_w{a}")
-            nc.sync.dma_start(tile[:].bitcast(I32), tab_words[a].rearrange("p t i -> p (t i)").bitcast(I32))
+        def load_table(kp):
+            tile = keep.tile([P, T], U32, name=f"tab_w{kp}", tag=f"tab_w{kp}")
+            nc.sync.dma_start(tile[:].bitcast(I32), tab_words[kp].rearrange("p t i -> p (t i)").bitcast(I32))
             return tile
 
-        def load_w1(a, b, tag):
+        def load_w1(kp, rp, tag):
             tile = keep.tile([P, PACK, PASS], F32, name="w1_raw", tag=tag)
-            rows = w1[a * PASS : (a + 1) * PASS, b * PASS : (b + 1) * PASS]
+            rows = w1[kp * PASS : (kp + 1) * PASS, rp * PASS : (rp + 1) * PASS]
             nc.sync.dma_start(tile[:], rows.rearrange("(p j) c -> p j c", j=PACK))
             return tile
 
-        def load_w2(b):
-            tile = keep.tile([P, 2, 2 * PASS], U8, name="w2_raw")
-            cols = w2_words[:, :, 2 * b * PASS : 2 * (b + 1) * PASS]
-            nc.sync.dma_start(tile[:].bitcast(I32), cols.rearrange("a p c -> p a c").bitcast(I32))
-            return tile
-
-        def load_wo(b):
-            tile = keep.tile([P, PACK, N], F32, name="wo_raw", tag=f"stage{b}")
-            rows = wo[b * PASS : (b + 1) * PASS, :].rearrange("(g t i) n -> t g i n", t=PACK, i=8)
+        def load_wo(rp, tag):
+            tile = keep.tile([P, PACK, N], F32, name="wo_raw", tag=tag)
+            rows = wo[rp * PASS : (rp + 1) * PASS, :].rearrange("(g t i) n -> t g i n", t=PACK, i=RUN)
             for t in range(PACK):
                 nc.sync.dma_start(tile[:, t, :], rows[t])
             return tile
 
+        tab_s = keep.tile([P, T], U8, name="tab_s", tag="stage0")
+        nc.vector.memset(tab_s[:].bitcast(I32), 0)
         gain_rows = keep.tile([P, P], F32, name="gain_rows", tag="tab_w1")
         nc.vector.memset(gain_rows[:], 0.0)
-        for b in range(2):
+        for rp in range(2):
             nc.gpsimd.dma_start(
-                gain_rows[PACK * b : PACK * (b + 1), :].rearrange("t (g i) -> t g i", i=8),
-                gain[b * PASS : (b + 1) * PASS].rearrange("(g t i) -> t g i", t=PACK, i=8),
+                gain_rows[PACK * rp : PACK * (rp + 1), :].rearrange("t (g i) -> t g i", i=RUN),
+                gain[rp * PASS : (rp + 1) * PASS].rearrange("(g t i) -> t g i", t=PACK, i=RUN),
             )
         ident = keep.tile([P, P], F32, name="ident")
         make_identity(nc, ident[:])
-        tab_s = keep.tile([P, T], U8, name="tab_s", tag="stage0")
-        nc.vector.memset(tab_s[:].bitcast(I32), 0)
-        for q in range(4):
-            nc.scalar.dma_start(tab_s[32 * q : 32 * q + 8, :].bitcast(I32), tab_scales[:, 4 * q : 4 * q + 4, :].bitcast(I32))
+        for q in range(QUADS):
+            nc.scalar.dma_start(
+                tab_s[32 * q : 32 * q + 8, :].bitcast(I32), tab_scales[:, 4 * q : 4 * q + 4, :].bitcast(I32)
+            )
         w2_s_raw = keep.tile([P, 2, H], U8, name="w2_s_raw")
         nc.vector.memset(w2_s_raw[:].bitcast(I32), 0)
-        for q in range(4):
+        for q in range(QUADS):
             nc.gpsimd.dma_start(
                 w2_s_raw[32 * q : 32 * q + 4, :, :].bitcast(I32),
-                w2_scales[:, 4 * q : 4 * q + 4, :].rearrange("a r c -> r a c").bitcast(I32),
+                w2_scales[:, 4 * q : 4 * q + 4, :].rearrange("kp s c -> s kp c").bitcast(I32),
             )
-        v_s1 = keep.tile([P, S], U8, name="v_s1", align_bytes=64)
-        nc.vector.memset(v_s1[:].bitcast(I32), 0)
+        v_s_moved = keep.tile([P, S], U8, name="v_s_moved", align_bytes=64)
+        nc.vector.memset(v_s_moved[:].bitcast(I32), 0)
 
         offs_t = load_list(offs, "offs_t")
-        pos1_t = load_list(pos1, "pos1_t")
-        pos2_t = load_list(pos2, "pos2_t")
-        pos3_t = load_list(pos3, "pos3_t")
-        pos4_t = load_list(pos4, "pos4_t")
+        pair_lists = (load_list(pos1, "pos1_t"), load_list(pos2, "pos2_t"))
+        bed_lists = (load_list(pos3, "pos3_t"), load_list(pos4, "pos4_t"))
         tab_w = [load_table(0)]
         w1_raw = {(0, 0): load_w1(0, 0, "first"), (1, 0): load_w1(1, 0, "stage1")}
-        w2_raw = [load_w2(0)]
-        wo_raw = []
+        w2_raw = keep.tile([P, 2, 2 * H], U8, name="w2_raw")
+        nc.sync.dma_start(w2_raw[:].bitcast(I32), w2_words.rearrange("kp p c -> p kp c").bitcast(I32))
 
         gain_ps = psum.tile([P, BANK], F32, name="bank")
         nc.tensor.transpose(gain_ps[:, :P], gain_rows[:], ident[:])
-        gain_t = keep.tile([P, 8], F32, name="gain_t")
-        nc.scalar.copy(gain_t[:], gain_ps[:, :8])
+        gain_t = keep.tile([P, ROW_TILES], F32, name="gain_t")
+        nc.vector.tensor_copy(gain_t[:], gain_ps[:, :ROW_TILES])
         tab_w.append(load_table(1))
 
-        v_w = [keep.tile([P, S], U32, name=f"v_w{a}", align_bytes=64) for a in range(2)]
+        v_w = [keep.tile([P, S], U32, name=f"v_w{kp}", align_bytes=64) for kp in range(2)]
         nc.vector.tensor_copy(v_w[0][:], tab_w[0][:].indirect(offs_t[:]))
-        v_s0 = keep.tile([P, S], U8, name="v_s0", align_bytes=64)
-        nc.vector.tensor_copy(v_s0[:], tab_s[:].indirect(offs_t[:]))
-        for q in range(4):
-            nc.sync.dma_start(v_s1[32 * q : 32 * q + 4, :].bitcast(I32), v_s0[32 * q + 4 : 32 * q + 8, :].bitcast(I32))
-        v_s = [v_s0, v_s1]
-
-        w1_c, w1_s, w2_c = {}, {}, {}
-
-        def prepare_w1(a, b):
-            grouped = ring.tile([P, PACK, PASS], BF16, name="w1_grouped", align_bytes=64)
-            src = w1_raw[a, b][:].rearrange("p j (g t u i) -> p t g u j i", t=PACK, u=2, i=4)
-            dst = grouped[:].rearrange("p t (g u i j) -> p t g u j i", u=2, i=4, j=PACK)
-            for t in range(PACK):
-                nc.scalar.copy(dst[:, t], src[:, t])
-            codes = keep.tile([P, PASS], U32, name=f"w1_c{a}{b}", align_bytes=64)
-            scales = keep.tile([P, PASS], U8, name=f"w1_s{a}{b}", align_bytes=64)
-            nc.vector.quantize_mx(codes[:].bitcast(FP8X4), scales[:], grouped[:].rearrange("p t c -> p (t c)"))
-            w1_c[a, b], w1_s[a, b] = codes, scales
-
-        def prepare_w2(b):
-            tile = keep.tile([P, 2, 2 * PASS], U8, name=f"w2_c{b}", align_bytes=64)
-            nc.vector.tensor_copy(
-                tile[:].bitcast(I32).rearrange("p a (t g w) -> p a t g w", t=PACK, w=4),
-                w2_raw[b][:].bitcast(I32).rearrange("p a (g t w) -> p a t g w", t=PACK, w=4),
+        v_s_both = keep.tile([P, S], U8, name="v_s_both", align_bytes=64)
+        nc.vector.tensor_copy(v_s_both[:], tab_s[:].indirect(offs_t[:]))
+        for q in range(QUADS):
+            nc.sync.dma_start(
+                v_s_moved[32 * q : 32 * q + 4, :].bitcast(I32), v_s_both[32 * q + 4 : 32 * q + 8, :].bitcast(I32)
             )
-            w2_c[b] = tile
+        v_planes = {"a": (v_s_both[:], v_s_both[4:, :]), "b": (v_s_both[:], v_s_moved[:])}
 
-        wo_c = [keep.tile([P, N], U32, name=f"wo_c{b}", align_bytes=64) for b in range(2)]
-        wo_s = [keep.tile([P, N], U8, name=f"wo_s{b}", align_bytes=64) for b in range(2)]
+        w1_q, wo_q = {}, {}
 
-        def prepare_wo(b, part):
+        def quantise_w1(rp, pieces, grouped):
+            dst = grouped[:].rearrange("p n (g u e j) -> p n g u j e", e=LINE, u=RUN // LINE, j=PACK)
+            for n, (kp, t) in enumerate(pieces):
+                src = w1_raw[kp, rp][:].rearrange("p j (g t u e) -> p t g u j e", t=PACK, u=RUN // LINE, e=LINE)
+                nc.scalar.copy(dst[:, n], src[:, t])
+            suffix = f"{rp}{pieces[0][0]}{pieces[0][1]}"
+            codes = keep.tile([P, len(pieces) * P], U32, name="w1_c" + suffix, align_bytes=64)
+            scales = keep.tile([P, len(pieces) * P], U8, name="w1_s" + suffix, align_bytes=64)
+            nc.vector.quantize_mx(codes[:].bitcast(FP8X4), scales[:], grouped[:].rearrange("p n c -> p (n c)"))
+            for n, (kp, t) in enumerate(pieces):
+                cols = slice(n * P, (n + 1) * P)
+                w1_q[PACK * rp + t, kp] = (codes[:, cols].bitcast(FP8X4), scales[:, cols])
+
+        def round_wo(rp, part):
             cols = slice(part * WO_COLS, (part + 1) * WO_COLS)
-            grouped = ring.tile([P, WO_COLS, PACK], BF16, name="wo_grouped", align_bytes=64)
+            grouped = paced([P, WO_COLS, PACK], BF16)
             nc.scalar.copy(
-                grouped[:].rearrange("p (c i) t -> p c t i", i=4),
-                wo_raw[b][:, :, cols].rearrange("p t (c i) -> p c t i", i=4),
+                grouped[:].rearrange("p (c e) t -> p c t e", e=LINE),
+                wo_raw[rp][:, :, cols].rearrange("p t (c e) -> p c t e", e=LINE),
             )
-            nc.vector.quantize_mx(
-                wo_c[b][:, cols].bitcast(FP8X4), wo_s[b][:, cols], grouped[:].rearrange("p c t -> p (c t)")
-            )
+            return grouped
+
+        def quantise_wo(rp, part, grouped, codes):
+            scales = keep.tile([P, WO_COLS], U8, name=f"wo_s{rp}{part}", align_bytes=64)
+            nc.vector.quantize_mx(codes.bitcast(FP8X4), scales[:], grouped[:].rearrange("p c t -> p (c t)"))
+            for n in range(WO_COLS // P):
+                cols = slice(n * P, (n + 1) * P)
+                wo_q[part * WO_COLS // P + n, rp] = (codes[:, cols].bitcast(FP8X4), scales[:, cols])
 
         w2_s = keep.tile([P, 2, H], U8, name="w2_s", align_bytes=64)
         nc.vector.tensor_copy(
-            w2_s[:].bitcast(I32).rearrange("p a (b t g w) -> p (a b) t g w", b=2, t=PACK, w=2),
-            w2_s_raw[:].bitcast(I32).rearrange("p a (b g t w) -> p (a b) t g w", b=2, t=PACK, w=2),
+            w2_s[:].bitcast(I32).rearrange("p kp (rp t g w) -> p (kp rp) t g w", rp=2, t=PACK, w=2),
+            w2_s_raw[:].bitcast(I32).rearrange("p kp (rp g t w) -> p (kp rp) t g w", rp=2, t=PACK, w=2),
         )
-        prepare_w1(0, 0)
-        prepare_w1(1, 0)
-        prepare_w2(0)
-        for a in range(2):
-            w1_raw[a, 1] = load_w1(a, 1, f"stage{a}")
-        w2_raw.append(load_w2(1))
+        for kp in range(2):
+            grouped = ring.tile([P, PACK, PASS], BF16, name="w1_grouped", align_bytes=64)
+            quantise_w1(0, [(kp, t) for t in range(PACK)], grouped)
+        w2_c = keep.tile([P, 2, 2 * H], U8, name="w2_c", align_bytes=64)
+        nc.vector.tensor_copy(
+            w2_c[:].bitcast(I32).rearrange("p kp (rp t g w) -> p (kp rp) t g w", rp=2, t=PACK, w=4),
+            w2_raw[:].bitcast(I32).rearrange("p kp (rp g t w) -> p (kp rp) t g w", rp=2, t=PACK, w=4),
+        )
         for half in range(2):
             nc.vector.tensor_copy(
-                v_w[1][:, half * BANK : (half + 1) * BANK], tab_w[1][:].indirect(offs_t[:, half * 32 : (half + 1) * 32])
+                v_w[1][:, half * BANK : (half + 1) * BANK],
+                tab_w[1][:].indirect(offs_t[:, half * BANK // 16 : (half + 1) * BANK // 16]),
             )
+        w1_raw[0, 1] = load_w1(0, 1, "stage0")
+        w1_raw[1, 1] = load_w1(1, 1, "first")
+        wo_raw = (load_wo(0, "stage1"), load_wo(1, "tab_w1"))
 
-        def operands(r, a):
-            b, t = divmod(r, PACK)
-            cols = slice(t * P, (t + 1) * P)
-            first = (w1_c[a, b][:, cols].bitcast(FP8X4), w1_s[a, b][:, cols])
-            second = (w2_c[b][:, a, 2 * t * P : 2 * (t + 1) * P].bitcast(FP4X4), w2_s[:, a, r * P : (r + 1) * P])
-            return first, second
+        def weight(which, r, kp):
+            if which == "a":
+                return w1_q[r, kp]
+            return w2_c[:, kp, 2 * r * P : 2 * (r + 1) * P].bitcast(FP4X4), w2_s[:, kp, r * P : (r + 1) * P]
 
-        def reading(r, half, which):
+        def reading(which, r, half):
             bank = psum.tile([P, BANK], F32, name="bank")
-            if turned(r, half):
-                for piece in range(BANK // P):
-                    js = slice(half * BANK + piece * P, half * BANK + (piece + 1) * P)
-                    for a in range(2):
-                        codes, scales = operands(r, a)[which]
-                        nc.tensor.matmul_mx(
-                            bank[:, piece * P : (piece + 1) * P], lhsT=v_w[a][:, js].bitcast(FP8X4), lhsT_scale=v_s[a][:, js],
-                            rhs=codes, rhs_scale=scales, start=a == 0, stop=a == 1,
-                        )
-            else:
+            if r < PLAIN_TILES:
                 js = slice(half * BANK, (half + 1) * BANK)
-                for a in range(2):
-                    codes, scales = operands(r, a)[which]
+                for kp in range(2):
+                    codes, scales = weight(which, r, kp)
                     nc.tensor.matmul_mx(
                         bank[:], lhsT=codes, lhsT_scale=scales,
-                        rhs=v_w[a][:, js].bitcast(FP8X4), rhs_scale=v_s[a][:, js], start=a == 0, stop=a == 1,
+                        rhs=v_w[kp][:, js].bitcast(FP8X4), rhs_scale=v_planes[which][kp][:, js],
+                        start=kp == 0, stop=kp == 1,
                     )
+            else:
+                for piece in range(BANK // P):
+                    js = slice(half * BANK + piece * P, half * BANK + (piece + 1) * P)
+                    for kp in range(2):
+                        codes, scales = weight(which, r, kp)
+                        nc.tensor.matmul_mx(
+                            bank[:, piece * P : (piece + 1) * P],
+                            lhsT=v_w[kp][:, js].bitcast(FP8X4), lhsT_scale=v_planes[which][kp][:, js],
+                            rhs=codes, rhs_scale=scales, start=kp == 0, stop=kp == 1,
+                        )
             return bank
 
-        def products(r, half):
+        def two_terms(r, half):
             bent = ring.tile([P, BANK], F32, name="bent", bufs=4)
-            size = ring.tile([P, BANK], F32, name="size", bufs=4)
-            a_ps = reading(r, half, 0)
-            b_ps = reading(r, half, 1)
+            size = paced([P, BANK], F32)
+            a_ps = reading("a", r, half)
+            b_ps = reading("b", r, half)
             nc.scalar.activation(bent[:], a_ps[:], ACT.Tanh)
             nc.scalar.activation(size[:], a_ps[:], ACT.Abs)
-            if turned(r, half):
-                nc.vector.tensor_tensor(bent[:], b_ps[:], bent[:], ALU.mult)
-            else:
+            if r < PLAIN_TILES:
                 nc.vector.scalar_tensor_tensor(bent[:], b_ps[:], gain_t[:, r : r + 1], bent[:], ALU.mult, ALU.mult)
+            else:
+                nc.vector.tensor_tensor(bent[:], b_ps[:], bent[:], ALU.mult)
             return bent, size
 
-        def add_terms(r, half, h, bent, size):
-            js = slice(half * BANK, (half + 1) * BANK)
-            if turned(r, half):
+        def add_terms(r, half, bent, size):
+            h_half = h[r][:, half * BANK : (half + 1) * BANK]
+            if r < PLAIN_TILES:
+                nc.vector.scalar_tensor_tensor(h_half, size[:], gain_t[:, r : r + 1], bent[:], ALU.mult, ALU.add)
+            else:
                 bank = psum.tile([P, BANK], F32, name="bank")
                 for piece in range(BANK // P):
                     cols = slice(piece * P, (piece + 1) * P)
                     nc.tensor.matmul(bank[:, cols], lhsT=size[:, cols], rhs=ident[:], is_transpose=True, start=True, stop=False)
                     nc.tensor.matmul(bank[:, cols], lhsT=bent[:, cols], rhs=ident[:], is_transpose=True, start=False, stop=True)
-                nc.scalar.activation(h[:, js], bank[:], ACT.Copy, scale=gain_t[:, r : r + 1])
-            else:
-                nc.vector.scalar_tensor_tensor(h[:, js], size[:], gain_t[:, r : r + 1], bent[:], ALU.mult, ALU.add)
+                nc.scalar.activation(h_half, bank[:], ACT.Copy, scale=gain_t[:, r : r + 1])
 
-        z_c, z_s = {}, {}
+        def pick_view(r, side):
+            rp, t = divmod(r, PACK)
+            if t == 0:
+                views[rp, side] = keep.tile([P, PACK, PAIRS], F32, name="view", tag=f"view{rp}{side}", align_bytes=64)
+            nc.vector.tensor_copy(views[rp, side][:, t, :], h[r][:].indirect(pair_lists[side][:]))
 
-        def weaker(root, shoot):
+        def weaker(rp):
             z = ring.tile([P, PAIRS, PACK], BF16, name="z", align_bytes=64)
             nc.vector.tensor_tensor(
-                z[:].rearrange("p (c i) t -> p c t i", i=4),
-                root[:].rearrange("p t (c i) -> p c t i", i=4),
-                shoot[:].rearrange("p t (c i) -> p c t i", i=4),
+                z[:].rearrange("p (c e) t -> p c t e", e=LINE),
+                views[rp, 0][:].rearrange("p t (c e) -> p c t e", e=LINE),
+                views[rp, 1][:].rearrange("p t (c e) -> p c t e", e=LINE),
                 ALU.min,
             )
             return z
 
-        def quantise_z(b, z):
-            codes = keep.tile([P, PAIRS], U32, name=f"z_c{b}", align_bytes=64)
-            scales = keep.tile([P, PAIRS], U8, name=f"z_s{b}", align_bytes=64)
+        def quantise_z(rp, z):
+            codes = keep.tile([P, PAIRS], U32, name=f"z_c{rp}", align_bytes=64)
+            scales = keep.tile([P, PAIRS], U8, name=f"z_s{rp}", align_bytes=64)
             nc.vector.quantize_mx(codes[:].bitcast(FP8X4), scales[:], z[:].rearrange("p m t -> p (m t)"))
-            z_c[b], z_s[b] = codes, scales
+            return codes[:].bitcast(FP8X4), scales[:]
 
-        views, hs, terms = {}, {}, {}
-
-        def pick(r, side):
-            b, t = divmod(r, PACK)
-            if t == 0:
-                views[b, side] = ring.tile([P, PACK, PAIRS], F32, name=f"view{side}")
-            nc.vector.tensor_copy(views[b, side][:, t, :], hs[r][:].indirect((pos1_t, pos2_t)[side][:]))
-
-        z0 = None
-        for step in range(10):
+        views, h, terms, z_q = {}, {}, {}, []
+        for step in range(ROW_TILES + 2):
             for half in range(2):
-                if step < 8:
-                    terms[step, half] = products(step, half)
-                if 1 <= step < 9:
+                if step < ROW_TILES:
+                    terms[step, half] = two_terms(step, half)
+                if 1 <= step <= ROW_TILES:
                     if half == 0:
-                        hs[step - 1] = ring.tile([P, S], F32, name="h", bufs=3)
-                    add_terms(step - 1, half, hs[step - 1], *terms[step - 1, half])
-                if 2 <= step:
-                    pick(step - 2, half)
-            if step == 6:
-                z0 = weaker(views[0, 0], views[0, 1])
-            if step == 7:
-                quantise_z(0, z0)
-            if step in (1, 2):
-                prepare_w1(step - 1, 1)
-                wo_raw.append(load_wo(step - 1))
-            if step == 2:
-                prepare_w2(1)
-            if 3 <= step < 9:
-                prepare_wo(*divmod(step - 3, 3))
-        quantise_z(1, weaker(views[1, 0], views[1, 1]))
+                        h[step - 1] = ring.tile([P, S], F32, name="h", bufs=3)
+                    add_terms(step - 1, half, *terms[step - 1, half])
+                if step >= 2:
+                    pick_view(step - 2, half)
+            if step == PACK + 2:
+                z_first = weaker(0)
+            if step == PACK + 3:
+                z_q.append(quantise_z(0, z_first))
+            if PACK <= step + W1_AHEAD < ROW_TILES:
+                quantise_w1(1, [(kp, step + W1_AHEAD - PACK) for kp in range(2)], paced([P, 2, PASS], BF16))
+            if ROW_TILES - 2 <= step < ROW_TILES:
+                rp = step - (ROW_TILES - 2)
+                wo_codes = keep.tile([P, WO_COLS], U32, name=f"wo_c{rp}", align_bytes=64)
+                quantise_wo(rp, 0, round_wo(rp, 0), wo_codes[:])
+            if step == ROW_TILES:
+                late = [(rp, part, round_wo(rp, part)) for part in range(1, N // WO_COLS) for rp in range(2)]
+        z_q.append(quantise_z(1, weaker(1)))
+        late_codes = keep.tile([P, len(late), WO_COLS], U32, name="late_codes", tag="view10", align_bytes=64)
+        for n, (rp, part, rounded) in enumerate(late):
+            quantise_wo(rp, part, rounded, late_codes[:, n, :])
 
-        for n in range(N // P):
-            cols = slice(n * P, (n + 1) * P)
+        y = []
+        for n in range(OUT_TILES):
             y_ps = psum.tile([P, BANK], F32, name="bank")
-            for b in range(2):
+            for rp in range(2):
                 nc.tensor.matmul_mx(
-                    y_ps[:], lhsT=wo_c[b][:, cols].bitcast(FP8X4), lhsT_scale=wo_s[b][:, cols],
-                    rhs=z_c[b][:].bitcast(FP8X4), rhs_scale=z_s[b][:], start=b == 0, stop=b == 1,
+                    y_ps[:], lhsT=wo_q[n, rp][0], lhsT_scale=wo_q[n, rp][1],
+                    rhs=z_q[rp][0], rhs_scale=z_q[rp][1], start=rp == 0, stop=rp == 1,
                 )
-            y = ring.tile([P, PAIRS], F32, name="y", bufs=3)
-            nc.scalar.copy(y[:], y_ps[:])
-            left = ring.tile([P, OUTS], F32, name="left")
-            right = ring.tile([P, OUTS], F32, name="right")
-            nc.vector.tensor_copy(left[:], y[:].indirect(pos3_t[:]))
-            nc.vector.tensor_copy(right[:], y[:].indirect(pos4_t[:]))
+            y.append(keep.tile([P, PAIRS], F32, name=f"y{n}"))
+            nc.scalar.copy(y[n][:], y_ps[:])
+
+        def neighbour(n, side):
+            tile = ring.tile([P, OUTS], F32, name=f"neighbour{side}")
+            nc.vector.tensor_copy(tile[:], y[n][:].indirect(bed_lists[side][:]))
+            return tile
+
+        left = {0: neighbour(0, 0)}
+        for n in range(OUT_TILES):
+            right = neighbour(n, 1)
+            if n + 1 < OUT_TILES:
+                left[n + 1] = neighbour(n + 1, 0)
             best = ring.tile([P, OUTS], F32, name="best", bufs=3)
-            nc.vector.tensor_tensor(best[:], left[:], right[:], ALU.max)
-            nc.sync.dma_start(out[cols, :], best[:])
+            nc.vector.tensor_tensor(best[:], left[n][:], right[:], ALU.max)
+            nc.sync.dma_start(out[n * P : (n + 1) * P, :], best[:])

from contextlib import ExitStack

import concourse.mybir as mybir
from concourse.masks import make_identity

K, T, S, H, PAIRS, OUTS, N = 1024, 4096, 1024, 1024, 512, 256, 768
FLOPS = 2 * (2 * K * H * S + H * N * PAIRS)

F32 = mybir.dt.float32
BF16 = mybir.dt.bfloat16
I32 = mybir.dt.int32
U32 = mybir.dt.uint32
U16 = mybir.dt.uint16
U8 = mybir.dt.uint8
FP8X4 = mybir.dt.float8_e4m3fn_x4
FP4X4 = mybir.dt.float4_e2m1fn_x4
ALU = mybir.AluOpType
ACT = mybir.ActivationFunctionType

P = 128
PACK = 4
PASS = P * PACK
RUN = 8
QUADS = 4
BANK = 512
LINE = 4
ROW_TILES = H // P
OUT_TILES = N // P
WO_COLS = 256
PLAIN_TILES = 2
W1_AHEAD = 2


def tile_list_seedling_lifting_gauge_kernel(
    tc, tab_words, tab_scales, w1, w2_words, w2_scales, gain, wo, offs, pos1, pos2, pos3, pos4, out
):
    nc = tc.nc
    with ExitStack() as ctx:
        lists = ctx.enter_context(tc.tile_pool(name="lists", bufs=1))
        keep = ctx.enter_context(tc.tile_pool(name="keep", bufs=1))
        ring = ctx.enter_context(tc.tile_pool(name="ring", bufs=2))
        psum = ctx.enter_context(tc.psum_pool(name="psum", bufs=8))


        def paced(shape, dtype):
            return ring.tile(shape, dtype, name="paced", bufs=5, align_bytes=64)

        def load_list(src, name):
            tile = lists.tile(list(src.shape), U16, name=name)
            nc.sync.dma_start(tile[:], src)
            return tile

        def load_table(kp):
            tile = keep.tile([P, T], U32, name=f"tab_w{kp}", tag=f"tab_w{kp}")
            nc.sync.dma_start(tile[:].bitcast(I32), tab_words[kp].rearrange("p t i -> p (t i)").bitcast(I32))
            return tile

        def load_w1(kp, rp, tag):
            tile = keep.tile([P, PACK, PASS], F32, name="w1_raw", tag=tag)
            rows = w1[kp * PASS : (kp + 1) * PASS, rp * PASS : (rp + 1) * PASS]
            nc.sync.dma_start(tile[:], rows.rearrange("(p j) c -> p j c", j=PACK))
            return tile

        def load_wo(rp, tag):
            tile = keep.tile([P, PACK, N], F32, name="wo_raw", tag=tag)
            rows = wo[rp * PASS : (rp + 1) * PASS, :].rearrange("(g t i) n -> t g i n", t=PACK, i=RUN)
            for t in range(PACK):
                nc.sync.dma_start(tile[:, t, :], rows[t])
            return tile

        tab_s = keep.tile([P, T], U8, name="tab_s", tag="stage0")
        nc.vector.memset(tab_s[:].bitcast(I32), 0)
        gain_rows = keep.tile([P, P], F32, name="gain_rows", tag="tab_w1")
        nc.vector.memset(gain_rows[:], 0.0)
        for rp in range(2):
            nc.gpsimd.dma_start(
                gain_rows[PACK * rp : PACK * (rp + 1), :].rearrange("t (g i) -> t g i", i=RUN),
                gain[rp * PASS : (rp + 1) * PASS].rearrange("(g t i) -> t g i", t=PACK, i=RUN),
            )
        ident = keep.tile([P, P], F32, name="ident")
        make_identity(nc, ident[:])
        for q in range(QUADS):
            nc.scalar.dma_start(
                tab_s[32 * q : 32 * q + 8, :].bitcast(I32), tab_scales[:, 4 * q : 4 * q + 4, :].bitcast(I32)
            )
        w2_s_raw = keep.tile([P, 2, H], U8, name="w2_s_raw")
        nc.vector.memset(w2_s_raw[:].bitcast(I32), 0)
        for q in range(QUADS):
            nc.gpsimd.dma_start(
                w2_s_raw[32 * q : 32 * q + 4, :, :].bitcast(I32),
                w2_scales[:, 4 * q : 4 * q + 4, :].rearrange("kp s c -> s kp c").bitcast(I32),
            )
        v_s_moved = keep.tile([P, S], U8, name="v_s_moved", align_bytes=64)
        nc.vector.memset(v_s_moved[:].bitcast(I32), 0)

        offs_t = load_list(offs, "offs_t")
        pair_lists = (load_list(pos1, "pos1_t"), load_list(pos2, "pos2_t"))
        bed_lists = (load_list(pos3, "pos3_t"), load_list(pos4, "pos4_t"))
        tab_w = [load_table(0)]
        w1_raw = {(0, 0): load_w1(0, 0, "first"), (1, 0): load_w1(1, 0, "stage1")}
        w2_raw = keep.tile([P, 2, 2 * H], U8, name="w2_raw")
        nc.sync.dma_start(w2_raw[:].bitcast(I32), w2_words.rearrange("kp p c -> p kp c").bitcast(I32))

        gain_ps = psum.tile([P, BANK], F32, name="bank")
        nc.tensor.transpose(gain_ps[:, :P], gain_rows[:], ident[:])
        gain_t = keep.tile([P, ROW_TILES], F32, name="gain_t")
        nc.vector.tensor_copy(gain_t[:], gain_ps[:, :ROW_TILES])
        tab_w.append(load_table(1))

        v_w = [keep.tile([P, S], U32, name=f"v_w{kp}", align_bytes=64) for kp in range(2)]
        nc.vector.tensor_copy(v_w[0][:], tab_w[0][:].indirect(offs_t[:]))
        v_s_both = keep.tile([P, S], U8, name="v_s_both", align_bytes=64)
        nc.vector.tensor_copy(v_s_both[:], tab_s[:].indirect(offs_t[:]))
        for q in range(QUADS):
            nc.sync.dma_start(
                v_s_moved[32 * q : 32 * q + 4, :].bitcast(I32), v_s_both[32 * q + 4 : 32 * q + 8, :].bitcast(I32)
            )
        v_planes = {"a": (v_s_both[:], v_s_both[4:, :]), "b": (v_s_both[:], v_s_moved[:])}

        w1_q, wo_q = {}, {}

        def quantise_w1(rp, pieces, grouped):
            dst = grouped[:].rearrange("p n (g u e j) -> p n g u j e", e=LINE, u=RUN // LINE, j=PACK)
            for n, (kp, t) in enumerate(pieces):
                src = w1_raw[kp, rp][:].rearrange("p j (g t u e) -> p t g u j e", t=PACK, u=RUN // LINE, e=LINE)
                nc.scalar.copy(dst[:, n], src[:, t])
            suffix = f"{rp}{pieces[0][0]}{pieces[0][1]}"
            codes = keep.tile([P, len(pieces) * P], U32, name="w1_c" + suffix, align_bytes=64)
            scales = keep.tile([P, len(pieces) * P], U8, name="w1_s" + suffix, align_bytes=64)
            nc.vector.quantize_mx(codes[:].bitcast(FP8X4), scales[:], grouped[:].rearrange("p n c -> p (n c)"))
            for n, (kp, t) in enumerate(pieces):
                cols = slice(n * P, (n + 1) * P)
                w1_q[PACK * rp + t, kp] = (codes[:, cols].bitcast(FP8X4), scales[:, cols])

        def round_wo(rp, part):
            cols = slice(part * WO_COLS, (part + 1) * WO_COLS)
            grouped = paced([P, WO_COLS, PACK], BF16)
            nc.scalar.copy(
                grouped[:].rearrange("p (c e) t -> p c t e", e=LINE),
                wo_raw[rp][:, :, cols].rearrange("p t (c e) -> p c t e", e=LINE),
            )
            return grouped

        def quantise_wo(rp, part, grouped, codes):
            scales = keep.tile([P, WO_COLS], U8, name=f"wo_s{rp}{part}", align_bytes=64)
            nc.vector.quantize_mx(codes.bitcast(FP8X4), scales[:], grouped[:].rearrange("p c t -> p (c t)"))
            for n in range(WO_COLS // P):
                cols = slice(n * P, (n + 1) * P)
                wo_q[part * WO_COLS // P + n, rp] = (codes[:, cols].bitcast(FP8X4), scales[:, cols])

        w2_s = keep.tile([P, 2, H], U8, name="w2_s", align_bytes=64)
        nc.vector.tensor_copy(
            w2_s[:].bitcast(I32).rearrange("p kp (rp t g w) -> p (kp rp) t g w", rp=2, t=PACK, w=2),
            w2_s_raw[:].bitcast(I32).rearrange("p kp (rp g t w) -> p (kp rp) t g w", rp=2, t=PACK, w=2),
        )
        for kp in range(2):
            grouped = ring.tile([P, PACK, PASS], BF16, name="w1_grouped", align_bytes=64)
            quantise_w1(0, [(kp, t) for t in range(PACK)], grouped)
        w2_c = keep.tile([P, 2, 2 * H], U8, name="w2_c", align_bytes=64)
        nc.vector.tensor_copy(
            w2_c[:].bitcast(I32).rearrange("p kp (rp t g w) -> p (kp rp) t g w", rp=2, t=PACK, w=4),
            w2_raw[:].bitcast(I32).rearrange("p kp (rp g t w) -> p (kp rp) t g w", rp=2, t=PACK, w=4),
        )
        for half in range(2):
            nc.vector.tensor_copy(
                v_w[1][:, half * BANK : (half + 1) * BANK],
                tab_w[1][:].indirect(offs_t[:, half * BANK // 16 : (half + 1) * BANK // 16]),
            )
        w1_raw[0, 1] = load_w1(0, 1, "stage0")
        w1_raw[1, 1] = load_w1(1, 1, "first")
        wo_raw = (load_wo(0, "stage1"), load_wo(1, "tab_w1"))

        def weight(which, r, kp):
            if which == "a":
                return w1_q[r, kp]
            return w2_c[:, kp, 2 * r * P : 2 * (r + 1) * P].bitcast(FP4X4), w2_s[:, kp, r * P : (r + 1) * P]

        def reading(which, r, half):
            bank = psum.tile([P, BANK], F32, name="bank")
            if r < PLAIN_TILES:
                js = slice(half * BANK, (half + 1) * BANK)
                for kp in range(2):
                    codes, scales = weight(which, r, kp)
                    nc.tensor.matmul_mx(
                        bank[:], lhsT=codes, lhsT_scale=scales,
                        rhs=v_w[kp][:, js].bitcast(FP8X4), rhs_scale=v_planes[which][kp][:, js],
                        start=kp == 0, stop=kp == 1,
                    )
            else:
                for piece in range(BANK // P):
                    js = slice(half * BANK + piece * P, half * BANK + (piece + 1) * P)
                    for kp in range(2):
                        codes, scales = weight(which, r, kp)
                        nc.tensor.matmul_mx(
                            bank[:, piece * P : (piece + 1) * P],
                            lhsT=v_w[kp][:, js].bitcast(FP8X4), lhsT_scale=v_planes[which][kp][:, js],
                            rhs=codes, rhs_scale=scales, start=kp == 0, stop=kp == 1,
                        )
            return bank

        def two_terms(r, half):
            bent = ring.tile([P, BANK], F32, name="bent", bufs=4)
            size = paced([P, BANK], F32)
            a_ps = reading("a", r, half)
            b_ps = reading("b", r, half)
            nc.scalar.activation(bent[:], a_ps[:], ACT.Tanh)
            nc.scalar.activation(size[:], a_ps[:], ACT.Abs)
            if r < PLAIN_TILES:
                nc.vector.scalar_tensor_tensor(bent[:], b_ps[:], gain_t[:, r : r + 1], bent[:], ALU.mult, ALU.mult)
            else:
                nc.vector.tensor_tensor(bent[:], b_ps[:], bent[:], ALU.mult)
            return bent, size

        def add_terms(r, half, bent, size):
            h_half = h[r][:, half * BANK : (half + 1) * BANK]
            if r < PLAIN_TILES:
                nc.vector.scalar_tensor_tensor(h_half, size[:], gain_t[:, r : r + 1], bent[:], ALU.mult, ALU.add)
            else:
                bank = psum.tile([P, BANK], F32, name="bank")
                for piece in range(BANK // P):
                    cols = slice(piece * P, (piece + 1) * P)
                    nc.tensor.matmul(bank[:, cols], lhsT=size[:, cols], rhs=ident[:], is_transpose=True, start=True, stop=False)
                    nc.tensor.matmul(bank[:, cols], lhsT=bent[:, cols], rhs=ident[:], is_transpose=True, start=False, stop=True)
                nc.scalar.activation(h_half, bank[:], ACT.Copy, scale=gain_t[:, r : r + 1])

        def pick_view(r, side):
            rp, t = divmod(r, PACK)
            if t == 0:
                views[rp, side] = keep.tile([P, PACK, PAIRS], F32, name="view", tag=f"view{rp}{side}", align_bytes=64)
            nc.vector.tensor_copy(views[rp, side][:, t, :], h[r][:].indirect(pair_lists[side][:]))

        def weaker(rp):
            z = ring.tile([P, PAIRS, PACK], BF16, name="z", align_bytes=64)
            nc.vector.tensor_tensor(
                z[:].rearrange("p (c e) t -> p c t e", e=LINE),
                views[rp, 0][:].rearrange("p t (c e) -> p c t e", e=LINE),
                views[rp, 1][:].rearrange("p t (c e) -> p c t e", e=LINE),
                ALU.min,
            )
            return z

        def quantise_z(rp, z):
            codes = keep.tile([P, PAIRS], U32, name=f"z_c{rp}", align_bytes=64)
            scales = keep.tile([P, PAIRS], U8, name=f"z_s{rp}", align_bytes=64)
            nc.vector.quantize_mx(codes[:].bitcast(FP8X4), scales[:], z[:].rearrange("p m t -> p (m t)"))
            return codes[:].bitcast(FP8X4), scales[:]

        views, h, terms, z_q = {}, {}, {}, []
        for step in range(ROW_TILES + 2):
            for half in range(2):
                if step < ROW_TILES:
                    terms[step, half] = two_terms(step, half)
                if 1 <= step <= ROW_TILES:
                    if half == 0:
                        h[step - 1] = ring.tile([P, S], F32, name="h", bufs=3)
                    add_terms(step - 1, half, *terms[step - 1, half])
                if step >= 2:
                    pick_view(step - 2, half)
            if step == PACK + 2:
                z_first = weaker(0)
            if step == PACK + 3:
                z_q.append(quantise_z(0, z_first))
            if PACK <= step + W1_AHEAD < ROW_TILES:
                quantise_w1(1, [(kp, step + W1_AHEAD - PACK) for kp in range(2)], paced([P, 2, PASS], BF16))
            if ROW_TILES - 2 <= step < ROW_TILES:
                rp = step - (ROW_TILES - 2)
                wo_codes = keep.tile([P, WO_COLS], U32, name=f"wo_c{rp}", align_bytes=64)
                quantise_wo(rp, 0, round_wo(rp, 0), wo_codes[:])
            if step == ROW_TILES:
                late = [(rp, part, round_wo(rp, part)) for part in range(1, N // WO_COLS) for rp in range(2)]
        z_q.append(quantise_z(1, weaker(1)))
        late_codes = keep.tile([P, len(late), WO_COLS], U32, name="late_codes", tag="view10", align_bytes=64)
        for n, (rp, part, rounded) in enumerate(late):
            quantise_wo(rp, part, rounded, late_codes[:, n, :])

        y = []
        for n in range(OUT_TILES):
            y_ps = psum.tile([P, BANK], F32, name="bank")
            for rp in range(2):
                nc.tensor.matmul_mx(
                    y_ps[:], lhsT=wo_q[n, rp][0], lhsT_scale=wo_q[n, rp][1],
                    rhs=z_q[rp][0], rhs_scale=z_q[rp][1], start=rp == 0, stop=rp == 1,
                )
            y.append(keep.tile([P, PAIRS], F32, name=f"y{n}"))
            nc.scalar.copy(y[n][:], y_ps[:])

        def neighbour(n, side):
            tile = ring.tile([P, OUTS], F32, name=f"neighbour{side}")
            nc.vector.tensor_copy(tile[:], y[n][:].indirect(bed_lists[side][:]))
            return tile

        left = {0: neighbour(0, 0)}
        for n in range(OUT_TILES):
            right = neighbour(n, 1)
            if n + 1 < OUT_TILES:
                left[n + 1] = neighbour(n + 1, 0)
            best = ring.tile([P, OUTS], F32, name="best", bufs=3)
            nc.vector.tensor_tensor(best[:], left[n][:], right[:], ALU.max)
            nc.sync.dma_start(out[n * P : (n + 1) * P, :], best[:])
